import numpy as np
import ml_dtypes

BF16 = ml_dtypes.bfloat16


def bf(x):
    return np.asarray(x, np.float32).astype(BF16)


def f32(x):
    return np.asarray(x, np.float32)


def f64(x):
    return np.asarray(x).astype(np.float64)


def striped(idx):
    return np.tile(idx.reshape(-1, 16).T, (8, 1))


S, K, M, N, V, D = 512, 512, 512, 128, 16, 32


def setup_inputs():
    return {"base": bf(np.random.standard_normal((M, S))), "x": bf(np.random.standard_normal((K, N))), "w": bf(1.5 * np.random.standard_normal((K, M)) / np.sqrt(K)), "s": f32(0.5 + np.random.random_sample((M, 1))), "offs": striped(np.random.permutation(S)[:N])}


def reference(base, x, w, s, offs):
    idx = offs[:16].T.reshape(-1)
    z = f64(base).copy()
    z[:, idx] += f64(w).T @ f64(x)
    z = z * f64(s)
    u = z.reshape(M, V, D)
    u = u - u.max(axis=2, keepdims=True)
    u = np.exp(u)
    u = u / u.sum(axis=2, keepdims=True)
    return u.reshape(M, S)

@@ -1,0 +1,80 @@
+import concourse.mybir as mybir
+from concourse.masks import make_identity
+
+P = 128
+S = 512
+K = 512
+M = 512
+N = 128
+D = 32
+V = S // D
+KB = K // P
+MB = M // P
+
+FLOPS = 2 * K * M * N
+
+BF16, F32, U16 = mybir.dt.bfloat16, mybir.dt.float32, mybir.dt.uint16
+Act, Alu, X = mybir.ActivationFunctionType, mybir.AluOpType, mybir.AxisListType.X
+
+
+def tile_rows_rescore_kernel(tc, base, x, w, s, offs, out):
+    nc = tc.nc
+    with (
+        tc.tile_pool(name="held", bufs=1) as held,
+        tc.tile_pool(name="work", bufs=MB) as work,
+        tc.psum_pool(name="psum", bufs=1) as psum,
+    ):
+        base_t = held.tile([P, MB, S], BF16, name="base_t")
+        offs_t = held.tile([P, N // 16], U16, name="offs_t")
+        x_t = held.tile([P, KB, N], BF16, name="x_t")
+        w_t = held.tile([P, KB, M], BF16, name="w_t")
+        s_t = held.tile([P, MB], F32, name="s_t")
+        nc.sync.dma_start(base_t[:], base.rearrange("(a p) n -> p a n", p=P))
+        nc.sync.dma_start(offs_t[:], offs)
+        nc.sync.dma_start(x_t[:], x.rearrange("(p b) n -> p b n", b=KB))
+        nc.sync.dma_start(w_t[:], w.rearrange("(p b) m -> p b m", b=KB))
+        nc.sync.dma_start(s_t[:], s.rearrange("(a p) o -> p (a o)", p=P))
+
+        ident = held.tile([P, P], BF16, name="ident")
+        make_identity(nc, ident[:])
+
+        warm = held.tile([P, 1], F32, name="warm")
+        nc.vector.memset(warm[:], 0.0)
+        warm_out = held.tile([P, 1], F32, name="warm_out")
+        nc.scalar.activation(warm_out[:], warm[:], Act.Exp)
+
+        z = [psum.tile([P, S], F32, name=f"z{a}") for a in range(MB)]
+        for a in range(MB):
+            nc.tensor.matmul(z[a][:], ident[:], base_t[:, a, :], start=True, stop=False)
+
+        for a in range(MB):
+            for b in range(KB):
+                nc.tensor.matmul(
+                    z[a][:].indirect(offs_t[:]),
+                    w_t[:, b, a * P : (a + 1) * P],
+                    x_t[:, b, :],
+                    start=False,
+                    stop=(b == KB - 1),
+                )
+
+        out_v = out.rearrange("(a p) n -> a p n", p=P)
+        for a in range(MB):
+            z_slates = z[a][:].rearrange("p (v d) -> p v d", d=D)
+            t = work.tile([P, V, D], F32, name="t")
+            nc.scalar.activation(t[:].rearrange("p v d -> p (v d)"), z[a][:], Act.Copy, scale=s_t[:, a : a + 1])
+            top = work.tile([P, V], F32, name="top")
+            nc.vector.reduce_max(top[:], t[:], axis=X)
+            below = work.tile([P, V, D], F32, name="below")
+            nc.vector.scalar_tensor_tensor(
+                below[:], z_slates, s_t[:, a : a + 1], top[:].unsqueeze(2).to_broadcast([P, V, D]), Alu.mult, Alu.subtract
+            )
+            e = work.tile([P, V, D], F32, name="e")
+            nc.scalar.activation(e[:], below[:], Act.Exp)
+            total = work.tile([P, V], F32, name="total")
+            nc.vector.reduce_sum(total[:], e[:], axis=X)
+            share = work.tile([P, V], F32, name="share")
+            nc.vector.reciprocal(share[:], total[:])
+            o = work.tile([P, V, D], F32, name="o")
+            divider = nc.vector if a == MB - 1 else nc.gpsimd
+            divider.tensor_tensor(o[:], e[:], share[:].unsqueeze(2).to_broadcast([P, V, D]), Alu.mult)
+            nc.sync.dma_start(out_v[a], o[:].rearrange("p v d -> p (v d)"))

@@ -9,7 +9,9 @@ N = 128
 D = 32
 V = S // D
 KB = K // P
-MB = M // P
+HALVES = 2
+R = M // (P * HALVES)
+MH = M // HALVES
 
 FLOPS = 2 * K * M * N
 
@@ -19,62 +21,81 @@ Act, Alu, X = mybir.ActivationFunctionType, mybir.AluOpType, mybir.AxisListType.
 
 def tile_rows_rescore_kernel(tc, base, x, w, s, offs, out):
     nc = tc.nc
+    windows = [(h, r) for h in range(HALVES) for r in range(R)]
     with (
         tc.tile_pool(name="held", bufs=1) as held,
-        tc.tile_pool(name="work", bufs=MB) as work,
+        tc.tile_pool(name="work", bufs=len(windows)) as work,
         tc.psum_pool(name="psum", bufs=1) as psum,
     ):
-        base_t = held.tile([P, MB, S], BF16, name="base_t")
-        offs_t = held.tile([P, N // 16], U16, name="offs_t")
+        base_v = base.rearrange("(h p r) n -> h p r n", h=HALVES, r=R)
+        out_v = out.rearrange("(h p r) n -> h r p n", h=HALVES, r=R)
+        w_v = w.rearrange("(p b) m -> p b m", b=KB)
+
+        base_t = [held.tile([P, R, S], BF16, name=f"base_{h}") for h in range(HALVES)]
+        w_t = [held.tile([P, KB, MH], BF16, name=f"w_{h}") for h in range(HALVES)]
         x_t = held.tile([P, KB, N], BF16, name="x_t")
-        w_t = held.tile([P, KB, M], BF16, name="w_t")
-        s_t = held.tile([P, MB], F32, name="s_t")
-        nc.sync.dma_start(base_t[:], base.rearrange("(a p) n -> p a n", p=P))
+        s_t = held.tile([P, HALVES, R], F32, name="s_t")
+        offs_t = held.tile([P, N // 16], U16, name="offs_t")
+        for h in range(HALVES):
+            nc.sync.dma_start(base_t[h][:], base_v[h])
         nc.sync.dma_start(offs_t[:], offs)
         nc.sync.dma_start(x_t[:], x.rearrange("(p b) n -> p b n", b=KB))
-        nc.sync.dma_start(w_t[:], w.rearrange("(p b) m -> p b m", b=KB))
-        nc.sync.dma_start(s_t[:], s.rearrange("(a p) o -> p (a o)", p=P))
+        nc.sync.dma_start(w_t[0][:], w_v[:, :, 0:MH])
+        nc.sync.dma_start(s_t[:], s.rearrange("(h p r) o -> p h (r o)", h=HALVES, r=R))
+        nc.sync.dma_start(w_t[1][:], w_v[:, :, MH:M])
 
         ident = held.tile([P, P], BF16, name="ident")
         make_identity(nc, ident[:])
 
-        warm = held.tile([P, 1], F32, name="warm")
-        nc.vector.memset(warm[:], 0.0)
-        warm_out = held.tile([P, 1], F32, name="warm_out")
-        nc.scalar.activation(warm_out[:], warm[:], Act.Exp)
+        early = held.tile([P, 1], F32, name="early")
+        nc.vector.memset(early[:], 0.0)
+        early_out = held.tile([P, 1], F32, name="early_out")
+        nc.scalar.activation(early_out[:], early[:], Act.Exp)
 
-        z = [psum.tile([P, S], F32, name=f"z{a}") for a in range(MB)]
-        for a in range(MB):
-            nc.tensor.matmul(z[a][:], ident[:], base_t[:, a, :], start=True, stop=False)
+        z = [psum.tile([P, S], F32, name=f"z_{h}_{r}") for h, r in windows]
+        for i, (h, r) in enumerate(windows):
+            nc.tensor.matmul(z[i][:], ident[:], base_t[h][:, r, :], start=True, stop=False)
 
-        for a in range(MB):
+        for i, (h, r) in enumerate(windows):
             for b in range(KB):
                 nc.tensor.matmul(
-                    z[a][:].indirect(offs_t[:]),
-                    w_t[:, b, a * P : (a + 1) * P],
+                    z[i][:].indirect(offs_t[:]),
+                    w_t[h][:, b, r::R],
                     x_t[:, b, :],
                     start=False,
                     stop=(b == KB - 1),
                 )
 
-        out_v = out.rearrange("(a p) n -> a p n", p=P)
-        for a in range(MB):
-            z_slates = z[a][:].rearrange("p (v d) -> p v d", d=D)
+        for i, (h, r) in enumerate(windows):
+            s_i = s_t[:, h, r : r + 1]
             t = work.tile([P, V, D], F32, name="t")
-            nc.scalar.activation(t[:].rearrange("p v d -> p (v d)"), z[a][:], Act.Copy, scale=s_t[:, a : a + 1])
-            top = work.tile([P, V], F32, name="top")
-            nc.vector.reduce_max(top[:], t[:], axis=X)
-            below = work.tile([P, V, D], F32, name="below")
-            nc.vector.scalar_tensor_tensor(
-                below[:], z_slates, s_t[:, a : a + 1], top[:].unsqueeze(2).to_broadcast([P, V, D]), Alu.mult, Alu.subtract
-            )
+            nc.scalar.activation(t[:].rearrange("p v d -> p (v d)"), z[i][:], Act.Copy, scale=s_i)
+            neg_top = work.tile([P, V], F32, name="neg_top")
+            nc.vector.reduce_max(neg_top[:], t[:], axis=X, negate=True)
+
             e = work.tile([P, V, D], F32, name="e")
-            nc.scalar.activation(e[:], below[:], Act.Exp)
             total = work.tile([P, V], F32, name="total")
-            nc.vector.reduce_sum(total[:], e[:], axis=X)
+            if i % 2 == 0:
+                below = work.tile([P, V, D], F32, name="below")
+                nc.vector.scalar_tensor_tensor(
+                    below[:],
+                    z[i][:].rearrange("p (v d) -> p v d", d=D),
+                    s_i,
+                    neg_top[:].unsqueeze(2).to_broadcast([P, V, D]),
+                    Alu.mult,
+                    Alu.add,
+                )
+                nc.scalar.activation(e[:], below[:], Act.Exp)
+                nc.vector.reduce_sum(total[:], e[:], axis=X)
+            else:
+                for v in range(V):
+                    nc.scalar.activation(
+                        e[:, v, :], t[:, v, :], Act.Exp, bias=neg_top[:, v : v + 1], accum_out=total[:, v : v + 1]
+                    )
+
             share = work.tile([P, V], F32, name="share")
             nc.vector.reciprocal(share[:], total[:])
             o = work.tile([P, V, D], F32, name="o")
-            divider = nc.vector if a == MB - 1 else nc.gpsimd
+            divider = nc.vector if i == len(windows) - 1 else nc.gpsimd
             divider.tensor_tensor(o[:], e[:], share[:].unsqueeze(2).to_broadcast([P, V, D]), Alu.mult)
-            nc.sync.dma_start(out_v[a], o[:].rearrange("p v d -> p (v d)"))
+            nc.sync.dma_start(out_v[h, r], o[:].rearrange("p v d -> p (v d)"))

@@ -13,6 +13,8 @@ HALVES = 2
 R = M // (P * HALVES)
 MH = M // HALVES
 
+WARM_UP = 4
+
 FLOPS = 2 * K * M * N
 
 BF16, F32, U16 = mybir.dt.bfloat16, mybir.dt.float32, mybir.dt.uint16
@@ -52,6 +54,12 @@ def tile_rows_rescore_kernel(tc, base, x, w, s, offs, out):
         early_out = held.tile([P, 1], F32, name="early_out")
         nc.scalar.activation(early_out[:], early[:], Act.Exp)
 
+        zeros = held.tile([P, S], BF16, name="zeros")
+        nc.vector.memset(zeros[:], 0.0)
+        spare = psum.tile([P, S], F32, name="spare")
+        for i in range(WARM_UP):
+            nc.tensor.matmul(spare[:], zeros[:, 0:P], zeros[:], start=True, stop=True)
+
         z = [psum.tile([P, S], F32, name=f"z_{h}_{r}") for h, r in windows]
         for i, (h, r) in enumerate(windows):
             nc.tensor.matmul(z[i][:], ident[:], base_t[h][:, r, :], start=True, stop=False)
@@ -66,13 +74,14 @@ def tile_rows_rescore_kernel(tc, base, x, w, s, offs, out):
                     stop=(b == KB - 1),
                 )
 
+        t, neg_top = [], []
         for i, (h, r) in enumerate(windows):
-            s_i = s_t[:, h, r : r + 1]
-            t = work.tile([P, V, D], F32, name="t")
-            nc.scalar.activation(t[:].rearrange("p v d -> p (v d)"), z[i][:], Act.Copy, scale=s_i)
-            neg_top = work.tile([P, V], F32, name="neg_top")
-            nc.vector.reduce_max(neg_top[:], t[:], axis=X, negate=True)
+            t.append(work.tile([P, V, D], F32, name="t"))
+            nc.scalar.activation(t[i][:].rearrange("p v d -> p (v d)"), z[i][:], Act.Copy, scale=s_t[:, h, r : r + 1])
+            neg_top.append(work.tile([P, V], F32, name="neg_top"))
+            nc.vector.reduce_max(neg_top[i][:], t[i][:], axis=X, negate=True)
 
+        for i, (h, r) in enumerate(windows):
             e = work.tile([P, V, D], F32, name="e")
             total = work.tile([P, V], F32, name="total")
             if i % 2 == 0:
@@ -80,22 +89,28 @@ def tile_rows_rescore_kernel(tc, base, x, w, s, offs, out):
                 nc.vector.scalar_tensor_tensor(
                     below[:],
                     z[i][:].rearrange("p (v d) -> p v d", d=D),
-                    s_i,
-                    neg_top[:].unsqueeze(2).to_broadcast([P, V, D]),
+                    s_t[:, h, r : r + 1],
+                    neg_top[i][:].unsqueeze(2).to_broadcast([P, V, D]),
                     Alu.mult,
                     Alu.add,
                 )
                 nc.scalar.activation(e[:], below[:], Act.Exp)
                 nc.vector.reduce_sum(total[:], e[:], axis=X)
+                parts = [slice(0, V)]
             else:
                 for v in range(V):
                     nc.scalar.activation(
-                        e[:, v, :], t[:, v, :], Act.Exp, bias=neg_top[:, v : v + 1], accum_out=total[:, v : v + 1]
+                        e[:, v, :], t[i][:, v, :], Act.Exp, bias=neg_top[i][:, v : v + 1], accum_out=total[:, v : v + 1]
                     )
+                parts = [slice(0, V // 2), slice(V // 2, V)]
 
             share = work.tile([P, V], F32, name="share")
-            nc.vector.reciprocal(share[:], total[:])
             o = work.tile([P, V, D], F32, name="o")
-            divider = nc.vector if i == len(windows) - 1 else nc.gpsimd
-            divider.tensor_tensor(o[:], e[:], share[:].unsqueeze(2).to_broadcast([P, V, D]), Alu.mult)
+            divider = nc.gpsimd if h == 0 else nc.vector
+            for part in parts:
+                n = part.stop - part.start
+                nc.vector.reciprocal(share[:, part], total[:, part])
+                divider.tensor_tensor(
+                    o[:, part, :], e[:, part, :], share[:, part].unsqueeze(2).to_broadcast([P, n, D]), Alu.mult
+                )
             nc.sync.dma_start(out_v[h, r], o[:].rearrange("p v d -> p (v d)"))

@@ -83,32 +83,17 @@ def tile_rows_rescore_kernel(tc, base, x, w, s, offs, out):
 
         for i, (h, r) in enumerate(windows):
             e = work.tile([P, V, D], F32, name="e")
-            total = work.tile([P, V], F32, name="total")
-            if i % 2 == 0:
-                below = work.tile([P, V, D], F32, name="below")
-                nc.vector.scalar_tensor_tensor(
-                    below[:],
-                    z[i][:].rearrange("p (v d) -> p v d", d=D),
-                    s_t[:, h, r : r + 1],
-                    neg_top[i][:].unsqueeze(2).to_broadcast([P, V, D]),
-                    Alu.mult,
-                    Alu.add,
-                )
-                nc.scalar.activation(e[:], below[:], Act.Exp)
-                nc.vector.reduce_sum(total[:], e[:], axis=X)
-                parts = [slice(0, V)]
-            else:
-                for v in range(V):
-                    nc.scalar.activation(
-                        e[:, v, :], t[i][:, v, :], Act.Exp, bias=neg_top[i][:, v : v + 1], accum_out=total[:, v : v + 1]
-                    )
-                parts = [slice(0, V // 2), slice(V // 2, V)]
+            for v in range(V):
+                nc.scalar.activation(e[:, v, :], t[i][:, v, :], Act.Exp, bias=neg_top[i][:, v : v + 1])
 
+            divider = nc.gpsimd if h == 0 else nc.vector
+            n = V // 2 if i == len(windows) - 1 else V
+            total = work.tile([P, V], F32, name="total")
             share = work.tile([P, V], F32, name="share")
             o = work.tile([P, V, D], F32, name="o")
-            divider = nc.gpsimd if h == 0 else nc.vector
-            for part in parts:
-                n = part.stop - part.start
+            for v in range(0, V, n):
+                part = slice(v, v + n)
+                nc.vector.reduce_sum(total[:, part], e[:, part, :], axis=X)
                 nc.vector.reciprocal(share[:, part], total[:, part])
                 divider.tensor_tensor(
                     o[:, part, :], e[:, part, :], share[:, part].unsqueeze(2).to_broadcast([P, n, D]), Alu.mult

@@ -26,6 +26,7 @@ def tile_rows_rescore_kernel(tc, base, x, w, s, offs, out):
     windows = [(h, r) for h in range(HALVES) for r in range(R)]
     with (
         tc.tile_pool(name="held", bufs=1) as held,
+        tc.tile_pool(name="scaled", bufs=2) as scaled,
         tc.tile_pool(name="work", bufs=len(windows)) as work,
         tc.psum_pool(name="psum", bufs=1) as psum,
     ):
@@ -74,28 +75,30 @@ def tile_rows_rescore_kernel(tc, base, x, w, s, offs, out):
                     stop=(b == KB - 1),
                 )
 
-        t, neg_top = [], []
         for i, (h, r) in enumerate(windows):
-            t.append(work.tile([P, V, D], F32, name="t"))
-            nc.scalar.activation(t[i][:].rearrange("p v d -> p (v d)"), z[i][:], Act.Copy, scale=s_t[:, h, r : r + 1])
-            neg_top.append(work.tile([P, V], F32, name="neg_top"))
-            nc.vector.reduce_max(neg_top[i][:], t[i][:], axis=X, negate=True)
+            t = scaled.tile([P, V, D], F32, name="t")
+            nc.scalar.activation(t[:].rearrange("p v d -> p (v d)"), z[i][:], Act.Copy, scale=s_t[:, h, r : r + 1])
+            neg_top = work.tile([P, V], F32, name="neg_top")
+            nc.vector.reduce_max(neg_top[:], t[:], axis=X, negate=True)
 
-        for i, (h, r) in enumerate(windows):
             e = work.tile([P, V, D], F32, name="e")
             for v in range(V):
-                nc.scalar.activation(e[:, v, :], t[i][:, v, :], Act.Exp, bias=neg_top[i][:, v : v + 1])
+                nc.scalar.activation(e[:, v, :], t[:, v, :], Act.Exp, bias=neg_top[:, v : v + 1])
 
-            divider = nc.gpsimd if h == 0 else nc.vector
             n = V // 2 if i == len(windows) - 1 else V
             total = work.tile([P, V], F32, name="total")
             share = work.tile([P, V], F32, name="share")
             o = work.tile([P, V, D], F32, name="o")
-            for v in range(0, V, n):
-                part = slice(v, v + n)
+            for v0 in range(0, V, n):
+                part = slice(v0, v0 + n)
                 nc.vector.reduce_sum(total[:, part], e[:, part, :], axis=X)
                 nc.vector.reciprocal(share[:, part], total[:, part])
-                divider.tensor_tensor(
-                    o[:, part, :], e[:, part, :], share[:, part].unsqueeze(2).to_broadcast([P, n, D]), Alu.mult
-                )
-            nc.sync.dma_start(out_v[h, r], o[:].rearrange("p v d -> p (v d)"))
+                if h == 0 or r == R - 1:
+                    divider = nc.gpsimd if h == 0 else nc.vector
+                    divider.tensor_tensor(
+                        o[:, part, :], e[:, part, :], share[:, part].unsqueeze(2).to_broadcast([P, n, D]), Alu.mult
+                    )
+                else:
+                    for v in range(v0, v0 + n):
+                        nc.scalar.activation(o[:, v, :], e[:, v, :], Act.Copy, scale=share[:, v : v + 1])
+                nc.sync.dma_start(out_v[h, r][:, v0 * D : (v0 + n) * D], o[:, part, :].rearrange("p v d -> p (v d)"))

import concourse.mybir as mybir
from concourse.masks import make_identity

P = 128
S = 512
K = 512
M = 512
N = 128
D = 32
V = S // D
KB = K // P
HALVES = 2
R = M // (P * HALVES)
MH = M // HALVES

WARM_UP = 4

FLOPS = 2 * K * M * N

BF16, F32, U16 = mybir.dt.bfloat16, mybir.dt.float32, mybir.dt.uint16
Act, Alu, X = mybir.ActivationFunctionType, mybir.AluOpType, mybir.AxisListType.X


def tile_rows_rescore_kernel(tc, base, x, w, s, offs, out):
    nc = tc.nc
    windows = [(h, r) for h in range(HALVES) for r in range(R)]
    with (
        tc.tile_pool(name="held", bufs=1) as held,
        tc.tile_pool(name="scaled", bufs=2) as scaled,
        tc.tile_pool(name="work", bufs=len(windows)) as work,
        tc.psum_pool(name="psum", bufs=1) as psum,
    ):
        base_v = base.rearrange("(h p r) n -> h p r n", h=HALVES, r=R)
        out_v = out.rearrange("(h p r) n -> h r p n", h=HALVES, r=R)
        w_v = w.rearrange("(p b) m -> p b m", b=KB)

        base_t = [held.tile([P, R, S], BF16, name=f"base_{h}") for h in range(HALVES)]
        w_t = [held.tile([P, KB, MH], BF16, name=f"w_{h}") for h in range(HALVES)]
        x_t = held.tile([P, KB, N], BF16, name="x_t")
        s_t = held.tile([P, HALVES, R], F32, name="s_t")
        offs_t = held.tile([P, N // 16], U16, name="offs_t")
        for h in range(HALVES):
            nc.sync.dma_start(base_t[h][:], base_v[h])
        nc.sync.dma_start(offs_t[:], offs)
        nc.sync.dma_start(x_t[:], x.rearrange("(p b) n -> p b n", b=KB))
        nc.sync.dma_start(w_t[0][:], w_v[:, :, 0:MH])
        nc.sync.dma_start(s_t[:], s.rearrange("(h p r) o -> p h (r o)", h=HALVES, r=R))
        nc.sync.dma_start(w_t[1][:], w_v[:, :, MH:M])

        ident = held.tile([P, P], BF16, name="ident")
        make_identity(nc, ident[:])

        early = held.tile([P, 1], F32, name="early")
        nc.vector.memset(early[:], 0.0)
        early_out = held.tile([P, 1], F32, name="early_out")
        nc.scalar.activation(early_out[:], early[:], Act.Exp)

        zeros = held.tile([P, S], BF16, name="zeros")
        nc.vector.memset(zeros[:], 0.0)
        spare = psum.tile([P, S], F32, name="spare")
        for i in range(WARM_UP):
            nc.tensor.matmul(spare[:], zeros[:, 0:P], zeros[:], start=True, stop=True)

        z = [psum.tile([P, S], F32, name=f"z_{h}_{r}") for h, r in windows]
        for i, (h, r) in enumerate(windows):
            nc.tensor.matmul(z[i][:], ident[:], base_t[h][:, r, :], start=True, stop=False)

        for i, (h, r) in enumerate(windows):
            for b in range(KB):
                nc.tensor.matmul(
                    z[i][:].indirect(offs_t[:]),
                    w_t[h][:, b, r::R],
                    x_t[:, b, :],
                    start=False,
                    stop=(b == KB - 1),
                )

        for i, (h, r) in enumerate(windows):
            t = scaled.tile([P, V, D], F32, name="t")
            nc.scalar.activation(t[:].rearrange("p v d -> p (v d)"), z[i][:], Act.Copy, scale=s_t[:, h, r : r + 1])
            neg_top = work.tile([P, V], F32, name="neg_top")
            nc.vector.reduce_max(neg_top[:], t[:], axis=X, negate=True)

            e = work.tile([P, V, D], F32, name="e")
            for v in range(V):
                nc.scalar.activation(e[:, v, :], t[:, v, :], Act.Exp, bias=neg_top[:, v : v + 1])

            n = V // 2 if i == len(windows) - 1 else V
            total = work.tile([P, V], F32, name="total")
            share = work.tile([P, V], F32, name="share")
            o = work.tile([P, V, D], F32, name="o")
            for v0 in range(0, V, n):
                part = slice(v0, v0 + n)
                nc.vector.reduce_sum(total[:, part], e[:, part, :], axis=X)
                nc.vector.reciprocal(share[:, part], total[:, part])
                if h == 0 or r == R - 1:
                    divider = nc.gpsimd if h == 0 else nc.vector
                    divider.tensor_tensor(
                        o[:, part, :], e[:, part, :], share[:, part].unsqueeze(2).to_broadcast([P, n, D]), Alu.mult
                    )
                else:
                    for v in range(v0, v0 + n):
                        nc.scalar.activation(o[:, v, :], e[:, v, :], Act.Copy, scale=share[:, v : v + 1])
                nc.sync.dma_start(out_v[h, r][:, v0 * D : (v0 + n) * D], o[:, part, :].rearrange("p v d -> p (v d)"))
